import numpy as np
import ml_dtypes


def mxq(x, axis, fmt="e4m3"):
    dtype, down = {"e4m3": (ml_dtypes.float8_e4m3fn, 7), "e5m2": (ml_dtypes.float8_e5m2, 14)}[fmt]
    v = np.moveaxis(np.asarray(x, np.float32).astype(ml_dtypes.bfloat16).astype(np.float64), axis, -1)
    blocks = v.reshape(v.shape[:-1] + (-1, 32))
    amax = np.abs(blocks).max(-1, keepdims=True)
    byte = np.maximum(np.where(amax > 0, np.frexp(amax)[1] - 1 + 127, 0) - down, 1)
    scale = np.exp2(byte - 127.0)
    codes = (blocks / scale).astype(np.float32).astype(dtype).astype(np.float64)
    return np.moveaxis((codes * scale).reshape(v.shape), -1, axis)


WIDE = False


def mx_kscale(k):
    if not WIDE:
        return np.ones(k)
    levels = np.array([18, -18])
    if k % 512:
        return np.exp2(np.random.permutation(np.resize(levels, k // 32))).repeat(32)
    a = np.empty((k // 512, 16))
    for p in range(k // 512):
        a[p, :8] = np.random.permutation(np.resize(levels, 8))
        for g in range(8):
            far = levels[np.abs(levels - a[p, g]) >= 10]
            a[p, g + 8] = far[np.random.randint(len(far))]
    return np.exp2(a.ravel()).repeat(32)


def f64(x):
    return np.asarray(x).astype(np.float64)


def striped(idx):
    return np.tile(np.asarray(idx).reshape(-1, 16).T, (8, 1)).astype(np.uint16)


def unstriped(offs):
    return offs[:16].T.reshape(-1).astype(np.int64)


B, N, T, D, R = 1, 512, 2048, 512, 512


def setup_inputs():
    n = np.random.standard_normal
    idx = np.random.permutation(T)[:B * N]
    s = mx_kscale(D)[:, None]
    z = mx_kscale(R)[:, None]
    x = n((B, D, R))
    return {
        "xT": (x * s).astype(np.float32),
        "wT": (n((D, T)) * (1.00 / np.sqrt(D)) / s).astype(np.float32),
        "y": (2 * np.random.randint(0, 2, (B, R, N)) - 1).astype(np.float32),
        "wt": (np.random.uniform(0.5, 1.5, (B, R, 1)) * 1.0 / np.sqrt(R) * z).astype(np.float32),
        "xm": (x.transpose(0, 2, 1) / z).astype(np.float32),
        "offs": striped(idx),
    }


def reference(xT, wT, y, wt, xm, offs):
    idx = unstriped(offs)
    pick = lambda x: x[:, idx].reshape(x.shape[0], B, N).transpose(1, 0, 2)
    a = mxq(f64(xT), 1, "e4m3").transpose(0, 2, 1) @ mxq(pick(f64(wT)), 1, "e4m3")
    g = -f64(wt) * f64(y) * np.maximum(1.0 - f64(y) * a, 0.0)
    dw = mxq(f64(xm), 1, "e4m3").transpose(0, 2, 1) @ mxq(g, 1, "e5m2")
    gw = np.zeros((D, T))
    gw[:, idx] = dw.transpose(1, 0, 2).reshape(D, B * N)
    return gw

@@ -1,0 +1,179 @@
+from contextlib import ExitStack
+
+import concourse.mybir as mybir
+
+D, T, R, N = 512, 2048, 512, 512
+FLOPS = 2 * 2 * D * R * N
+
+F32 = mybir.dt.float32
+BF16 = mybir.dt.bfloat16
+U32 = mybir.dt.uint32
+U16 = mybir.dt.uint16
+U8 = mybir.dt.uint8
+E4M3 = mybir.dt.float8_e4m3fn_x4
+E5M2 = mybir.dt.float8_e5m2_x4
+COPY = mybir.ActivationFunctionType.Copy
+RELU = mybir.ActivationFunctionType.Relu
+MULT = mybir.AluOpType.mult
+
+P = 128
+PACK = 4
+HALF = N // 2
+QUART = N // 4
+M_SCALAR = 16
+
+
+def tile_attend_gsqh_w_kernel(tc, xT, wT, y, wt, xm, offs, out):
+    nc = tc.nc
+    with ExitStack() as ctx:
+        sb = ctx.enter_context(tc.tile_pool(name="sb", bufs=1))
+        ps = ctx.enter_context(tc.psum_pool(name="ps", bufs=1))
+
+        offsets = sb.tile([P, N // 16], U16, name="offsets")
+        wt_sb = sb.tile([P, PACK], F32, name="wt_sb")
+        planes = [sb.tile([P, T], F32, name=f"plane{j}") for j in range(PACK)]
+        x_raw = [sb.tile([P, PACK, R // 2], F32, name=f"x_raw{h}") for h in range(2)]
+        y_sb = [sb.tile([P, PACK, HALF], F32, name=f"y_sb{h}") for h in range(2)]
+        xm_raw = sb.tile([P, PACK, D], F32, name="xm_raw")
+
+        w_rows = wT.rearrange("(p j) c -> p j c", j=PACK)
+        x_rows = xT[0].rearrange("(p j) r -> p j r", j=PACK)
+        y_rows = y[0].rearrange("(p t) i -> p t i", t=PACK)
+        nc.sync.dma_start(planes[0][:], w_rows[:, 0, :])
+        nc.sync.dma_start(offsets[:], offs)
+        nc.sync.dma_start(wt_sb[:], wt[0].rearrange("(p t) o -> p (t o)", t=PACK))
+        for j in range(1, PACK):
+            nc.sync.dma_start(planes[j][:], w_rows[:, j, :])
+        for h in range(2):
+            nc.sync.dma_start(x_raw[h][:], x_rows[:, :, h * (R // 2) : (h + 1) * (R // 2)])
+        for h in range(2):
+            nc.sync.dma_start(y_sb[h][:], y_rows[:, :, h * HALF : (h + 1) * HALF])
+        nc.sync.dma_start(xm_raw[:], xm[0].rearrange("(p t) d -> p t d", t=PACK))
+
+        windows = [sb.tile([P, T], F32, name=f"window{b}") for b in range(D // P)]
+        for b in range(D // P):
+            nc.gpsimd.memset(windows[b][:], 0.0)
+
+        neg_wt = sb.tile([P, PACK], F32, name="neg_wt")
+        nc.scalar.activation(neg_wt[:], wt_sb[:], COPY, scale=-1.0)
+
+        def mx_tiles(label):
+            grouped = sb.tile([P, 512, PACK], BF16, name=f"{label}_bf", align_bytes=64)
+            codes = sb.tile([P, 512], U32, name=f"{label}_codes", align_bytes=64)
+            scales = sb.tile([P, 512], U8, name=f"{label}_scales", align_bytes=64)
+            return grouped, codes, scales
+
+        def quantize(tiles, c0, c1, fmt):
+            grouped, codes, scales = tiles
+            nc.vector.quantize_mx(
+                out=codes[:, c0:c1].bitcast(fmt),
+                scales=scales[:, c0:c1],
+                in_=grouped[:, c0:c1, :].rearrange("p c j -> p (c j)"),
+            )
+
+        w_mx, x_mx, g_mx, xm_mx = mx_tiles("w"), mx_tiles("x"), mx_tiles("g"), mx_tiles("xm")
+
+        for j in range(PACK):
+            nc.vector.tensor_copy(w_mx[0][:, :, j], planes[j][:].indirect(offsets[:]))
+        quantize(w_mx, 0, N, E4M3)
+
+        x_view = x_mx[0][:].rearrange("p (t m) j -> p m t j", t=PACK)
+        half_m = P // 2
+
+        def x_src(h):
+            return x_raw[h][:].rearrange("p j (m t) -> p m t j", t=PACK)
+
+        nc.scalar.copy(x_view[:, 0:half_m], x_src(0))
+        nc.vector.tensor_copy(x_view[:, half_m : P - M_SCALAR], x_src(1)[:, 0 : half_m - M_SCALAR])
+        nc.scalar.copy(x_view[:, P - M_SCALAR : P], x_src(1)[:, half_m - M_SCALAR : half_m])
+        quantize(x_mx, 0, R, E4M3)
+
+        scores = [ps.tile([P, PACK, QUART], F32, name=f"scores{q}") for q in range(4)]
+        wy = [sb.tile([P, PACK, HALF], F32, name=f"wy{h}") for h in range(2)]
+        margin = [sb.tile([P, PACK, QUART], F32, name=f"margin{q}") for q in range(4)]
+        slack = [sb.tile([P, PACK, QUART], F32, name=f"slack{q}") for q in range(4)]
+
+        def score(q):
+            cols = slice(q * QUART, (q + 1) * QUART)
+            for t in range(PACK):
+                rows = slice(t * P, (t + 1) * P)
+                nc.tensor.matmul_mx(
+                    out=scores[q][:, t, :],
+                    lhsT=x_mx[1][:, rows].bitcast(E4M3),
+                    lhsT_scale=x_mx[2][:, rows],
+                    rhs=w_mx[1][:, cols].bitcast(E4M3),
+                    rhs_scale=w_mx[2][:, cols],
+                    start=True,
+                    stop=True,
+                )
+
+        def in_half(tiles, q):
+            return tiles[q // 2][:, :, (q % 2) * QUART : (q % 2 + 1) * QUART]
+
+        def weigh(h):
+            for t in range(PACK):
+                nc.scalar.activation(wy[h][:, t, :], y_sb[h][:, t, :], COPY, scale=neg_wt[:, t : t + 1])
+
+        def hinge(q):
+            nc.vector.tensor_tensor(margin[q][:], scores[q][:], in_half(y_sb, q), MULT)
+            nc.scalar.activation(slack[q][:], margin[q][:], RELU, bias=1.0, scale=-1.0)
+
+        def gradient(q):
+            nc.vector.tensor_tensor(
+                g_mx[0][:, q * QUART : (q + 1) * QUART, :].rearrange("p (c e) t -> p c t e", e=2),
+                slack[q][:].rearrange("p t (c e) -> p c t e", e=2),
+                in_half(wy, q).rearrange("p t (c e) -> p c t e", e=2),
+                MULT,
+            )
+
+        def group_xm(b):
+            nc.scalar.copy(
+                xm_mx[0][:, b * P : (b + 1) * P, :].rearrange("p (c e) t -> p c t e", e=4),
+                xm_raw[:, :, b * P : (b + 1) * P].rearrange("p t (c e) -> p c t e", e=4),
+            )
+
+        for q in range(4):
+            score(q)
+        weigh(0)
+        hinge(0)
+        hinge(1)
+        weigh(1)
+        gradient(0)
+        hinge(2)
+        gradient(1)
+        hinge(3)
+        quantize(g_mx, 0, HALF, E5M2)
+        group_xm(0)
+        gradient(2)
+        gradient(3)
+        quantize(xm_mx, 0, P, E4M3)
+        quantize(g_mx, HALF, N, E5M2)
+        group_xm(1)
+
+        for b in range(D // P):
+            cols = slice(b * P, (b + 1) * P)
+            if b > 0:
+                quantize(xm_mx, b * P, (b + 1) * P, E4M3)
+            dw_ps = ps.tile([P, N], F32, name=f"dw_ps{b}")
+            nc.tensor.matmul_mx(
+                out=dw_ps[:],
+                lhsT=xm_mx[1][:, cols].bitcast(E4M3),
+                lhsT_scale=xm_mx[2][:, cols],
+                rhs=g_mx[1][:].bitcast(E5M2),
+                rhs_scale=g_mx[2][:],
+                start=True,
+                stop=True,
+            )
+            dw = sb.tile([P, N], F32, name=f"dw{b}")
+            pieces = 2 if b == 0 else 1
+            width = N // pieces
+            for s in range(pieces):
+                nc.scalar.copy(dw[:, s * width : (s + 1) * width], dw_ps[:, s * width : (s + 1) * width])
+            if b + 2 < D // P:
+                group_xm(b + 2)
+            for s in range(pieces):
+                nc.vector.tensor_copy(
+                    windows[b][:].indirect(offsets[:, s * width // 16 : (s + 1) * width // 16]),
+                    dw[:, s * width : (s + 1) * width],
+                )
+            nc.sync.dma_start(out[cols, :], windows[b][:])

@@ -15,12 +15,12 @@ E5M2 = mybir.dt.float8_e5m2_x4
 COPY = mybir.ActivationFunctionType.Copy
 RELU = mybir.ActivationFunctionType.Relu
 MULT = mybir.AluOpType.mult
+ADD = mybir.AluOpType.add
 
 P = 128
 PACK = 4
 HALF = N // 2
-QUART = N // 4
-M_SCALAR = 16
+BLOCKS = D // P
 
 
 def tile_attend_gsqh_w_kernel(tc, xT, wT, y, wt, xm, offs, out):
@@ -32,73 +32,73 @@ def tile_attend_gsqh_w_kernel(tc, xT, wT, y, wt, xm, offs, out):
         offsets = sb.tile([P, N // 16], U16, name="offsets")
         wt_sb = sb.tile([P, PACK], F32, name="wt_sb")
         planes = [sb.tile([P, T], F32, name=f"plane{j}") for j in range(PACK)]
-        x_raw = [sb.tile([P, PACK, R // 2], F32, name=f"x_raw{h}") for h in range(2)]
+        x_raw = sb.tile([P, PACK, R], F32, name="x_raw")
         y_sb = [sb.tile([P, PACK, HALF], F32, name=f"y_sb{h}") for h in range(2)]
-        xm_raw = sb.tile([P, PACK, D], F32, name="xm_raw")
+        xm_first = sb.tile([P, PACK, P], F32, name="xm_first", tag="shared")
+        xm_rest = sb.tile([P, PACK, D - P], F32, name="xm_rest")
 
         w_rows = wT.rearrange("(p j) c -> p j c", j=PACK)
-        x_rows = xT[0].rearrange("(p j) r -> p j r", j=PACK)
         y_rows = y[0].rearrange("(p t) i -> p t i", t=PACK)
         nc.sync.dma_start(planes[0][:], w_rows[:, 0, :])
         nc.sync.dma_start(offsets[:], offs)
         nc.sync.dma_start(wt_sb[:], wt[0].rearrange("(p t) o -> p (t o)", t=PACK))
         for j in range(1, PACK):
             nc.sync.dma_start(planes[j][:], w_rows[:, j, :])
-        for h in range(2):
-            nc.sync.dma_start(x_raw[h][:], x_rows[:, :, h * (R // 2) : (h + 1) * (R // 2)])
+        nc.sync.dma_start(x_raw[:], xT[0].rearrange("(p j) r -> p j r", j=PACK))
         for h in range(2):
             nc.sync.dma_start(y_sb[h][:], y_rows[:, :, h * HALF : (h + 1) * HALF])
-        nc.sync.dma_start(xm_raw[:], xm[0].rearrange("(p t) d -> p t d", t=PACK))
+        xm_rows = xm[0].rearrange("(p t) d -> p t d", t=PACK)
+        nc.sync.dma_start(xm_first[:], xm_rows[:, :, 0:P])
+        nc.sync.dma_start(xm_rest[:], xm_rows[:, :, P:D])
 
-        windows = [sb.tile([P, T], F32, name=f"window{b}") for b in range(D // P)]
-        for b in range(D // P):
-            nc.gpsimd.memset(windows[b][:], 0.0)
-
-        neg_wt = sb.tile([P, PACK], F32, name="neg_wt")
-        nc.scalar.activation(neg_wt[:], wt_sb[:], COPY, scale=-1.0)
-
-        def mx_tiles(label):
+        def mx_tiles(label, words):
             grouped = sb.tile([P, 512, PACK], BF16, name=f"{label}_bf", align_bytes=64)
-            codes = sb.tile([P, 512], U32, name=f"{label}_codes", align_bytes=64)
-            scales = sb.tile([P, 512], U8, name=f"{label}_scales", align_bytes=64)
+            codes = sb.tile([P, words], U32, name=f"{label}_codes", align_bytes=64)
+            scales = sb.tile([P, words], U8, name=f"{label}_scales", align_bytes=64)
             return grouped, codes, scales
 
-        def quantize(tiles, c0, c1, fmt):
+        def quantize(tiles, c0, c1, fmt, shift=0):
             grouped, codes, scales = tiles
             nc.vector.quantize_mx(
-                out=codes[:, c0:c1].bitcast(fmt),
-                scales=scales[:, c0:c1],
+                out=codes[:, shift + c0 : shift + c1].bitcast(fmt),
+                scales=scales[:, shift + c0 : shift + c1],
                 in_=grouped[:, c0:c1, :].rearrange("p c j -> p (c j)"),
             )
 
-        w_mx, x_mx, g_mx, xm_mx = mx_tiles("w"), mx_tiles("x"), mx_tiles("g"), mx_tiles("xm")
+        w_mx, x_mx, xm_mx = mx_tiles("w", N), mx_tiles("x", R), mx_tiles("xm", D)
+        g_mx = mx_tiles("g", HALF + N)
+
+        nc.gpsimd.memset(g_mx[1][:, 0:HALF], 0)
+        nc.gpsimd.memset(g_mx[2][:, 0:HALF], 0)
+        windows = [sb.tile([P, T], F32, name=f"window{b}") for b in range(BLOCKS)]
+        for b in range(BLOCKS):
+            engine = nc.vector if b < 2 else nc.gpsimd
+            engine.memset(windows[b][:], 0.0)
+
+        neg_wt = sb.tile([P, PACK], F32, name="neg_wt")
+        nc.scalar.activation(neg_wt[:], wt_sb[:], COPY, scale=-1.0)
 
         for j in range(PACK):
             nc.vector.tensor_copy(w_mx[0][:, :, j], planes[j][:].indirect(offsets[:]))
         quantize(w_mx, 0, N, E4M3)
 
-        x_view = x_mx[0][:].rearrange("p (t m) j -> p m t j", t=PACK)
-        half_m = P // 2
+        x_dst = x_mx[0][:].rearrange("p (t m) j -> p m j t", t=PACK)
+        x_src = x_raw[:].rearrange("p j (m t) -> p m j t", t=PACK)
+        nc.vector.tensor_copy(x_dst[:, :, :, 0:2], x_src[:, :, :, 0:2])
+        nc.scalar.copy(x_dst[:, :, :, 2:4], x_src[:, :, :, 2:4])
 
-        def x_src(h):
-            return x_raw[h][:].rearrange("p j (m t) -> p m t j", t=PACK)
-
-        nc.scalar.copy(x_view[:, 0:half_m], x_src(0))
-        nc.vector.tensor_copy(x_view[:, half_m : P - M_SCALAR], x_src(1)[:, 0 : half_m - M_SCALAR])
-        nc.scalar.copy(x_view[:, P - M_SCALAR : P], x_src(1)[:, half_m - M_SCALAR : half_m])
-        quantize(x_mx, 0, R, E4M3)
-
-        scores = [ps.tile([P, PACK, QUART], F32, name=f"scores{q}") for q in range(4)]
+        scores = {}
         wy = [sb.tile([P, PACK, HALF], F32, name=f"wy{h}") for h in range(2)]
-        margin = [sb.tile([P, PACK, QUART], F32, name=f"margin{q}") for q in range(4)]
-        slack = [sb.tile([P, PACK, QUART], F32, name=f"slack{q}") for q in range(4)]
+        margin = {}
+        slack = {}
 
-        def score(q):
-            cols = slice(q * QUART, (q + 1) * QUART)
-            for t in range(PACK):
-                rows = slice(t * P, (t + 1) * P)
+        def score(u, h):
+            cols = slice(h * HALF, (h + 1) * HALF)
+            scores[u, h] = ps.tile([P, 2, HALF], F32, name=f"scores{u}{h}", tag=f"bank{u}{h}")
+            for e in range(2):
+                rows = slice((2 * u + e) * P, (2 * u + e + 1) * P)
                 nc.tensor.matmul_mx(
-                    out=scores[q][:, t, :],
+                    out=scores[u, h][:, e, :],
                     lhsT=x_mx[1][:, rows].bitcast(E4M3),
                     lhsT_scale=x_mx[2][:, rows],
                     rhs=w_mx[1][:, cols].bitcast(E4M3),
@@ -107,73 +107,88 @@ def tile_attend_gsqh_w_kernel(tc, xT, wT, y, wt, xm, offs, out):
                     stop=True,
                 )
 
-        def in_half(tiles, q):
-            return tiles[q // 2][:, :, (q % 2) * QUART : (q % 2 + 1) * QUART]
-
         def weigh(h):
             for t in range(PACK):
-                nc.scalar.activation(wy[h][:, t, :], y_sb[h][:, t, :], COPY, scale=neg_wt[:, t : t + 1])
+                if h == 0:
+                    nc.scalar.activation(wy[h][:, t, :], y_sb[h][:, t, :], COPY, scale=neg_wt[:, t : t + 1])
+                else:
+                    nc.gpsimd.tensor_scalar(wy[h][:, t, :], y_sb[h][:, t, :], neg_wt[:, t : t + 1], 0.0, MULT, ADD)
 
-        def hinge(q):
-            nc.vector.tensor_tensor(margin[q][:], scores[q][:], in_half(y_sb, q), MULT)
-            nc.scalar.activation(slack[q][:], margin[q][:], RELU, bias=1.0, scale=-1.0)
+        def margins(u, h):
+            margin[u, h] = sb.tile([P, 2, HALF], F32, name=f"margin{u}{h}")
+            nc.vector.tensor_tensor(margin[u, h][:], scores[u, h][:], y_sb[h][:, 2 * u : 2 * u + 2, :], MULT)
 
-        def gradient(q):
+        def hinge(u, h):
+            nc.scalar.activation(slack[h][:, 2 * u : 2 * u + 2, :], margin[u, h][:], RELU, bias=1.0, scale=-1.0)
+
+        def gradient(h):
+            cols = slice(h * HALF, (h + 1) * HALF)
             nc.vector.tensor_tensor(
-                g_mx[0][:, q * QUART : (q + 1) * QUART, :].rearrange("p (c e) t -> p c t e", e=2),
-                slack[q][:].rearrange("p t (c e) -> p c t e", e=2),
-                in_half(wy, q).rearrange("p t (c e) -> p c t e", e=2),
+                g_mx[0][:, cols, :].rearrange("p (c e) t -> p c t e", e=2),
+                slack[h][:].rearrange("p t (c e) -> p c t e", e=2),
+                wy[h][:].rearrange("p t (c e) -> p c t e", e=2),
                 MULT,
             )
 
         def group_xm(b):
+            raw = xm_first[:] if b == 0 else xm_rest[:, :, (b - 1) * P : b * P]
             nc.scalar.copy(
                 xm_mx[0][:, b * P : (b + 1) * P, :].rearrange("p (c e) t -> p c t e", e=4),
-                xm_raw[:, :, b * P : (b + 1) * P].rearrange("p t (c e) -> p c t e", e=4),
+                raw.rearrange("p t (c e) -> p c t e", e=4),
             )
 
-        for q in range(4):
-            score(q)
-        weigh(0)
-        hinge(0)
-        hinge(1)
-        weigh(1)
-        gradient(0)
-        hinge(2)
-        gradient(1)
-        hinge(3)
-        quantize(g_mx, 0, HALF, E5M2)
-        group_xm(0)
-        gradient(2)
-        gradient(3)
-        quantize(xm_mx, 0, P, E4M3)
-        quantize(g_mx, HALF, N, E5M2)
-        group_xm(1)
-
-        for b in range(D // P):
+        def product(bank, b, c0):
             cols = slice(b * P, (b + 1) * P)
-            if b > 0:
-                quantize(xm_mx, b * P, (b + 1) * P, E4M3)
-            dw_ps = ps.tile([P, N], F32, name=f"dw_ps{b}")
             nc.tensor.matmul_mx(
-                out=dw_ps[:],
+                out=bank[:],
                 lhsT=xm_mx[1][:, cols].bitcast(E4M3),
                 lhsT_scale=xm_mx[2][:, cols],
-                rhs=g_mx[1][:].bitcast(E5M2),
-                rhs_scale=g_mx[2][:],
+                rhs=g_mx[1][:, c0 : c0 + N].bitcast(E5M2),
+                rhs_scale=g_mx[2][:, c0 : c0 + N],
                 start=True,
                 stop=True,
             )
-            dw = sb.tile([P, N], F32, name=f"dw{b}")
-            pieces = 2 if b == 0 else 1
-            width = N // pieces
-            for s in range(pieces):
-                nc.scalar.copy(dw[:, s * width : (s + 1) * width], dw_ps[:, s * width : (s + 1) * width])
-            if b + 2 < D // P:
-                group_xm(b + 2)
-            for s in range(pieces):
-                nc.vector.tensor_copy(
-                    windows[b][:].indirect(offsets[:, s * width // 16 : (s + 1) * width // 16]),
-                    dw[:, s * width : (s + 1) * width],
-                )
-            nc.sync.dma_start(out[cols, :], windows[b][:])
+
+        def scatter(b, values, s0, s1):
+            nc.vector.tensor_copy(windows[b][:].indirect(offsets[:, s0 // 16 : s1 // 16]), values)
+
+        quantize(x_mx, 0, 2 * P, E4M3)
+        quantize(x_mx, 2 * P, 4 * P, E4M3)
+        for h in range(2):
+            for u in range(2):
+                score(u, h)
+        weigh(0)
+        weigh(1)
+        slack[0] = sb.tile([P, PACK, HALF], F32, name="slack0")
+        for u in range(2):
+            margins(u, 0)
+            hinge(u, 0)
+        group_xm(0)
+        slack[1] = sb.tile([P, PACK, HALF], F32, name="slack1", tag="shared")
+        for u in range(2):
+            margins(u, 1)
+            hinge(u, 1)
+        gradient(0)
+        quantize(xm_mx, 0, P, E4M3)
+        quantize(g_mx, 0, HALF, E5M2, shift=HALF)
+        early_ps = ps.tile([P, N], F32, name="early_ps", tag="bank00")
+        product(early_ps, 0, 0)
+        early = sb.tile([P, HALF], F32, name="early")
+        nc.scalar.copy(early[:], early_ps[:, HALF:N])
+        group_xm(1)
+        gradient(1)
+        quantize(xm_mx, P, 2 * P, E4M3)
+        quantize(g_mx, HALF, N, E5M2, shift=HALF)
+        scatter(0, early[:], 0, HALF)
+
+        for b in range(BLOCKS):
+            if b > 1:
+                group_xm(b)
+                quantize(xm_mx, b * P, (b + 1) * P, E4M3)
+            dw_ps = ps.tile([P, N], F32, name=f"dw_ps{b}")
+            product(dw_ps, b, HALF)
+            s0 = HALF if b == 0 else 0
+            dw = sb.tile([P, N - s0], F32, name=f"dw{b}")
+            nc.scalar.copy(dw[:], dw_ps[:, s0:N])
+            scatter(b, dw[:], s0, N)
+            nc.sync.dma_start(out[b * P : (b + 1) * P, :], windows[b][:])

@@ -21,6 +21,7 @@ P = 128
 PACK = 4
 HALF = N // 2
 BLOCKS = D // P
+QUART = N // 4
 
 
 def tile_attend_gsqh_w_kernel(tc, xT, wT, y, wt, xm, offs, out):
@@ -34,21 +35,21 @@ def tile_attend_gsqh_w_kernel(tc, xT, wT, y, wt, xm, offs, out):
         planes = [sb.tile([P, T], F32, name=f"plane{j}") for j in range(PACK)]
         x_raw = sb.tile([P, PACK, R], F32, name="x_raw")
         y_sb = [sb.tile([P, PACK, HALF], F32, name=f"y_sb{h}") for h in range(2)]
-        xm_first = sb.tile([P, PACK, P], F32, name="xm_first", tag="shared")
+        xm_first = sb.tile([P, PACK, P], F32, name="xm_first")
         xm_rest = sb.tile([P, PACK, D - P], F32, name="xm_rest")
 
         w_rows = wT.rearrange("(p j) c -> p j c", j=PACK)
         y_rows = y[0].rearrange("(p t) i -> p t i", t=PACK)
         nc.sync.dma_start(planes[0][:], w_rows[:, 0, :])
         nc.sync.dma_start(offsets[:], offs)
-        nc.sync.dma_start(wt_sb[:], wt[0].rearrange("(p t) o -> p (t o)", t=PACK))
+        nc.scalar.dma_start(wt_sb[:], wt[0].rearrange("(p t) o -> p (t o)", t=PACK))
         for j in range(1, PACK):
             nc.sync.dma_start(planes[j][:], w_rows[:, j, :])
         nc.sync.dma_start(x_raw[:], xT[0].rearrange("(p j) r -> p j r", j=PACK))
-        for h in range(2):
-            nc.sync.dma_start(y_sb[h][:], y_rows[:, :, h * HALF : (h + 1) * HALF])
         xm_rows = xm[0].rearrange("(p t) d -> p t d", t=PACK)
         nc.sync.dma_start(xm_first[:], xm_rows[:, :, 0:P])
+        for h in range(2):
+            nc.sync.dma_start(y_sb[h][:], y_rows[:, :, h * HALF : (h + 1) * HALF])
         nc.sync.dma_start(xm_rest[:], xm_rows[:, :, P:D])
 
         def mx_tiles(label, words):
@@ -121,12 +122,12 @@ def tile_attend_gsqh_w_kernel(tc, xT, wT, y, wt, xm, offs, out):
         def hinge(u, h):
             nc.scalar.activation(slack[h][:, 2 * u : 2 * u + 2, :], margin[u, h][:], RELU, bias=1.0, scale=-1.0)
 
-        def gradient(h):
-            cols = slice(h * HALF, (h + 1) * HALF)
+        def gradient(q):
+            cols = slice((q % 2) * QUART, (q % 2 + 1) * QUART)
             nc.vector.tensor_tensor(
-                g_mx[0][:, cols, :].rearrange("p (c e) t -> p c t e", e=2),
-                slack[h][:].rearrange("p t (c e) -> p c t e", e=2),
-                wy[h][:].rearrange("p t (c e) -> p c t e", e=2),
+                g_mx[0][:, q * QUART : (q + 1) * QUART, :].rearrange("p (c e) t -> p c t e", e=2),
+                slack[q // 2][:, :, cols].rearrange("p t (c e) -> p c t e", e=2),
+                wy[q // 2][:, :, cols].rearrange("p t (c e) -> p c t e", e=2),
                 MULT,
             )
 
@@ -157,26 +158,29 @@ def tile_attend_gsqh_w_kernel(tc, xT, wT, y, wt, xm, offs, out):
         for h in range(2):
             for u in range(2):
                 score(u, h)
+        group_xm(0)
+        quantize(xm_mx, 0, P, E4M3)
         weigh(0)
         weigh(1)
         slack[0] = sb.tile([P, PACK, HALF], F32, name="slack0")
         for u in range(2):
             margins(u, 0)
             hinge(u, 0)
-        group_xm(0)
-        slack[1] = sb.tile([P, PACK, HALF], F32, name="slack1", tag="shared")
+        slack[1] = sb.tile([P, PACK, HALF], F32, name="slack1")
         for u in range(2):
             margins(u, 1)
             hinge(u, 1)
         gradient(0)
-        quantize(xm_mx, 0, P, E4M3)
-        quantize(g_mx, 0, HALF, E5M2, shift=HALF)
+        gradient(1)
+        quantize(g_mx, 0, QUART, E5M2, shift=HALF)
+        quantize(g_mx, QUART, HALF, E5M2, shift=HALF)
         early_ps = ps.tile([P, N], F32, name="early_ps", tag="bank00")
         product(early_ps, 0, 0)
         early = sb.tile([P, HALF], F32, name="early")
         nc.scalar.copy(early[:], early_ps[:, HALF:N])
         group_xm(1)
-        gradient(1)
+        gradient(2)
+        gradient(3)
         quantize(xm_mx, P, 2 * P, E4M3)
         quantize(g_mx, HALF, N, E5M2, shift=HALF)
         scatter(0, early[:], 0, HALF)
@@ -191,4 +195,6 @@ def tile_attend_gsqh_w_kernel(tc, xT, wT, y, wt, xm, offs, out):
             dw = sb.tile([P, N - s0], F32, name=f"dw{b}")
             nc.scalar.copy(dw[:], dw_ps[:, s0:N])
             scatter(b, dw[:], s0, N)
-            nc.sync.dma_start(out[b * P : (b + 1) * P, :], windows[b][:])
+            nc.sync.dma_start(out[b * P : (b + 1) * P, 0 : T // 2], windows[b][:, 0 : T // 2])
+            second = nc.scalar if b == BLOCKS - 1 else nc.sync
+            second.dma_start(out[b * P : (b + 1) * P, T // 2 : T], windows[b][:, T // 2 : T])

@@ -22,6 +22,7 @@ PACK = 4
 HALF = N // 2
 BLOCKS = D // P
 QUART = N // 4
+W_SCALAR = 192
 
 
 def tile_attend_gsqh_w_kernel(tc, xT, wT, y, wt, xm, offs, out):
@@ -79,14 +80,28 @@ def tile_attend_gsqh_w_kernel(tc, xT, wT, y, wt, xm, offs, out):
         neg_wt = sb.tile([P, PACK], F32, name="neg_wt")
         nc.scalar.activation(neg_wt[:], wt_sb[:], COPY, scale=-1.0)
 
-        for j in range(PACK):
-            nc.vector.tensor_copy(w_mx[0][:, :, j], planes[j][:].indirect(offsets[:]))
-        quantize(w_mx, 0, N, E4M3)
+        picked = sb.tile([P, PACK, N], F32, name="picked")
+        for j in range(PACK - 1):
+            nc.vector.tensor_copy(picked[:, j, :], planes[j][:].indirect(offsets[:]))
+        for h in range(2):
+            nc.vector.tensor_copy(
+                picked[:, PACK - 1, h * HALF : (h + 1) * HALF],
+                planes[PACK - 1][:].indirect(offsets[:, h * HALF // 16 : (h + 1) * HALF // 16]),
+            )
+
+        def interleaved(grouped, raw):
+            return grouped.rearrange("p (c e) j -> p c j e", e=4), raw.rearrange("p j (c e) -> p c j e", e=4)
+
+        nc.scalar.copy(*interleaved(w_mx[0][:, 0:W_SCALAR, :], picked[:, :, 0:W_SCALAR]))
+        nc.vector.tensor_copy(*interleaved(w_mx[0][:, W_SCALAR:HALF, :], picked[:, :, W_SCALAR:HALF]))
+        nc.vector.tensor_copy(*interleaved(w_mx[0][:, HALF:N, :], picked[:, :, HALF:N]))
+        quantize(w_mx, 0, HALF, E4M3)
 
         x_dst = x_mx[0][:].rearrange("p (t m) j -> p m j t", t=PACK)
         x_src = x_raw[:].rearrange("p j (m t) -> p m j t", t=PACK)
         nc.vector.tensor_copy(x_dst[:, :, :, 0:2], x_src[:, :, :, 0:2])
         nc.scalar.copy(x_dst[:, :, :, 2:4], x_src[:, :, :, 2:4])
+        quantize(w_mx, HALF, N, E4M3)
 
         scores = {}
         wy = [sb.tile([P, PACK, HALF], F32, name=f"wy{h}") for h in range(2)]

@@ -22,7 +22,7 @@ PACK = 4
 HALF = N // 2
 BLOCKS = D // P
 QUART = N // 4
-W_SCALAR = 192
+EARLY = 2
 
 
 def tile_attend_gsqh_w_kernel(tc, xT, wT, y, wt, xm, offs, out):
@@ -34,7 +34,7 @@ def tile_attend_gsqh_w_kernel(tc, xT, wT, y, wt, xm, offs, out):
         offsets = sb.tile([P, N // 16], U16, name="offsets")
         wt_sb = sb.tile([P, PACK], F32, name="wt_sb")
         planes = [sb.tile([P, T], F32, name=f"plane{j}") for j in range(PACK)]
-        x_raw = sb.tile([P, PACK, R], F32, name="x_raw")
+        x_raw = [sb.tile([P, PACK, R // 2], F32, name=f"x_raw{h}", tag=f"x_raw{h}", align_bytes=64) for h in range(2)]
         y_sb = [sb.tile([P, PACK, HALF], F32, name=f"y_sb{h}") for h in range(2)]
         xm_first = sb.tile([P, PACK, P], F32, name="xm_first")
         xm_rest = sb.tile([P, PACK, D - P], F32, name="xm_rest")
@@ -46,32 +46,40 @@ def tile_attend_gsqh_w_kernel(tc, xT, wT, y, wt, xm, offs, out):
         nc.scalar.dma_start(wt_sb[:], wt[0].rearrange("(p t) o -> p (t o)", t=PACK))
         for j in range(1, PACK):
             nc.sync.dma_start(planes[j][:], w_rows[:, j, :])
-        nc.sync.dma_start(x_raw[:], xT[0].rearrange("(p j) r -> p j r", j=PACK))
+        x_rows = xT[0].rearrange("(p j) r -> p j r", j=PACK)
+        for h in range(2):
+            nc.sync.dma_start(x_raw[h][:], x_rows[:, :, h * R // 2 : (h + 1) * R // 2])
         xm_rows = xm[0].rearrange("(p t) d -> p t d", t=PACK)
-        nc.sync.dma_start(xm_first[:], xm_rows[:, :, 0:P])
         for h in range(2):
             nc.sync.dma_start(y_sb[h][:], y_rows[:, :, h * HALF : (h + 1) * HALF])
+        nc.sync.dma_start(xm_first[:], xm_rows[:, :, 0:P])
         nc.sync.dma_start(xm_rest[:], xm_rows[:, :, P:D])
 
+        def grouped_tile(label, columns):
+            return sb.tile([P, columns, PACK], BF16, name=f"{label}_bf", align_bytes=64)
+
         def mx_tiles(label, words):
-            grouped = sb.tile([P, 512, PACK], BF16, name=f"{label}_bf", align_bytes=64)
             codes = sb.tile([P, words], U32, name=f"{label}_codes", align_bytes=64)
             scales = sb.tile([P, words], U8, name=f"{label}_scales", align_bytes=64)
-            return grouped, codes, scales
+            return codes, scales
 
-        def quantize(tiles, c0, c1, fmt, shift=0):
-            grouped, codes, scales = tiles
+        def quantize(grouped, tiles, c0, c1, fmt):
+            codes, scales = tiles
             nc.vector.quantize_mx(
-                out=codes[:, shift + c0 : shift + c1].bitcast(fmt),
-                scales=scales[:, shift + c0 : shift + c1],
-                in_=grouped[:, c0:c1, :].rearrange("p c j -> p (c j)"),
+                out=codes[:, c0:c1].bitcast(fmt),
+                scales=scales[:, c0:c1],
+                in_=grouped.rearrange("p c j -> p (c j)"),
             )
 
         w_mx, x_mx, xm_mx = mx_tiles("w", N), mx_tiles("x", R), mx_tiles("xm", D)
         g_mx = mx_tiles("g", HALF + N)
+        w_bf = [grouped_tile("w0", HALF)]
+        x_bf = [grouped_tile(f"x{u}", 2 * P) for u in range(2)]
+        xm_bf = [grouped_tile(f"xm{b}", P) for b in range(BLOCKS)]
+        g_bf = [grouped_tile(f"g{h}", HALF) for h in range(2)]
 
+        nc.gpsimd.memset(g_mx[0][:, 0:HALF], 0)
         nc.gpsimd.memset(g_mx[1][:, 0:HALF], 0)
-        nc.gpsimd.memset(g_mx[2][:, 0:HALF], 0)
         windows = [sb.tile([P, T], F32, name=f"window{b}") for b in range(BLOCKS)]
         for b in range(BLOCKS):
             engine = nc.vector if b < 2 else nc.gpsimd
@@ -81,44 +89,55 @@ def tile_attend_gsqh_w_kernel(tc, xT, wT, y, wt, xm, offs, out):
         nc.scalar.activation(neg_wt[:], wt_sb[:], COPY, scale=-1.0)
 
         picked = sb.tile([P, PACK, N], F32, name="picked")
-        for j in range(PACK - 1):
-            nc.vector.tensor_copy(picked[:, j, :], planes[j][:].indirect(offsets[:]))
-        for h in range(2):
-            nc.vector.tensor_copy(
-                picked[:, PACK - 1, h * HALF : (h + 1) * HALF],
-                planes[PACK - 1][:].indirect(offsets[:, h * HALF // 16 : (h + 1) * HALF // 16]),
-            )
 
-        def interleaved(grouped, raw):
-            return grouped.rearrange("p (c e) j -> p c j e", e=4), raw.rearrange("p j (c e) -> p c j e", e=4)
+        def gather(j, s0, s1):
+            nc.vector.tensor_copy(picked[:, j, s0:s1], planes[j][:].indirect(offsets[:, s0 // 16 : s1 // 16]))
 
-        nc.scalar.copy(*interleaved(w_mx[0][:, 0:W_SCALAR, :], picked[:, :, 0:W_SCALAR]))
-        nc.vector.tensor_copy(*interleaved(w_mx[0][:, W_SCALAR:HALF, :], picked[:, :, W_SCALAR:HALF]))
-        nc.vector.tensor_copy(*interleaved(w_mx[0][:, HALF:N, :], picked[:, :, HALF:N]))
-        quantize(w_mx, 0, HALF, E4M3)
+        def interleaved(h, j0, j1):
+            dst = w_bf[h][:, :, j0:j1].rearrange("p (c e) j -> p c j e", e=4)
+            src = picked[:, j0:j1, h * HALF : (h + 1) * HALF].rearrange("p j (c e) -> p c j e", e=4)
+            return dst, src
 
-        x_dst = x_mx[0][:].rearrange("p (t m) j -> p m j t", t=PACK)
-        x_src = x_raw[:].rearrange("p j (m t) -> p m j t", t=PACK)
-        nc.vector.tensor_copy(x_dst[:, :, :, 0:2], x_src[:, :, :, 0:2])
-        nc.scalar.copy(x_dst[:, :, :, 2:4], x_src[:, :, :, 2:4])
-        quantize(w_mx, HALF, N, E4M3)
+        gather(0, 0, N)
+        gather(1, 0, N)
+        nc.scalar.copy(*interleaved(0, 0, 2))
+        gather(2, 0, N)
+        gather(3, 0, HALF)
+        gather(3, HALF, N)
+        nc.vector.tensor_copy(*interleaved(0, 2, 4))
+        quantize(w_bf[0][:], w_mx, 0, HALF, E4M3)
+
+        def dealt(h, u):
+            dst = x_bf[u][:].rearrange("p (t m) j -> p m j t", t=2)[:, h * P // 2 : (h + 1) * P // 2]
+            src = x_raw[h][:].rearrange("p j (m t) -> p m j t", t=PACK)[:, :, :, 2 * u : 2 * u + 2]
+            return dst, src
+
+        for u in range(2):
+            nc.scalar.copy(*dealt(0, u))
+        for u in range(2):
+            nc.vector.tensor_copy(*dealt(1, u))
+        for u in range(2):
+            quantize(x_bf[u][:], x_mx, 2 * u * P, 2 * (u + 1) * P, E4M3)
+        w_bf.append(sb.tile([P, HALF, PACK], BF16, name="w1_bf", tag="x_raw0", align_bytes=64))
+        nc.scalar.copy(*interleaved(1, 0, PACK))
+        quantize(w_bf[1][:], w_mx, HALF, N, E4M3)
 
         scores = {}
         wy = [sb.tile([P, PACK, HALF], F32, name=f"wy{h}") for h in range(2)]
         margin = {}
         slack = {}
 
-        def score(u, h):
-            cols = slice(h * HALF, (h + 1) * HALF)
-            scores[u, h] = ps.tile([P, 2, HALF], F32, name=f"scores{u}{h}", tag=f"bank{u}{h}")
-            for e in range(2):
-                rows = slice((2 * u + e) * P, (2 * u + e + 1) * P)
+        def score(q):
+            cols = slice(q * QUART, (q + 1) * QUART)
+            scores[q] = ps.tile([P, PACK, QUART], F32, name=f"scores{q}", tag=f"bank{q}")
+            for t in range(PACK):
+                rows = slice(t * P, (t + 1) * P)
                 nc.tensor.matmul_mx(
-                    out=scores[u, h][:, e, :],
-                    lhsT=x_mx[1][:, rows].bitcast(E4M3),
-                    lhsT_scale=x_mx[2][:, rows],
-                    rhs=w_mx[1][:, cols].bitcast(E4M3),
-                    rhs_scale=w_mx[2][:, cols],
+                    out=scores[q][:, t, :],
+                    lhsT=x_mx[0][:, rows].bitcast(E4M3),
+                    lhsT_scale=x_mx[1][:, rows],
+                    rhs=w_mx[0][:, cols].bitcast(E4M3),
+                    rhs_scale=w_mx[1][:, cols],
                     start=True,
                     stop=True,
                 )
@@ -130,18 +149,20 @@ def tile_attend_gsqh_w_kernel(tc, xT, wT, y, wt, xm, offs, out):
                 else:
                     nc.gpsimd.tensor_scalar(wy[h][:, t, :], y_sb[h][:, t, :], neg_wt[:, t : t + 1], 0.0, MULT, ADD)
 
-        def margins(u, h):
-            margin[u, h] = sb.tile([P, 2, HALF], F32, name=f"margin{u}{h}")
-            nc.vector.tensor_tensor(margin[u, h][:], scores[u, h][:], y_sb[h][:, 2 * u : 2 * u + 2, :], MULT)
+        def margins(q):
+            cols = slice((q % 2) * QUART, (q % 2 + 1) * QUART)
+            margin[q] = sb.tile([P, PACK, QUART], F32, name=f"margin{q}")
+            nc.vector.tensor_tensor(margin[q][:], scores[q][:], y_sb[q // 2][:, :, cols], MULT)
 
-        def hinge(u, h):
-            nc.scalar.activation(slack[h][:, 2 * u : 2 * u + 2, :], margin[u, h][:], RELU, bias=1.0, scale=-1.0)
+        def hinge(q):
+            slack[q] = sb.tile([P, PACK, QUART], F32, name=f"slack{q}", tag=f"slack{q}")
+            nc.scalar.activation(slack[q][:], margin[q][:], RELU, bias=1.0, scale=-1.0)
 
         def gradient(q):
             cols = slice((q % 2) * QUART, (q % 2 + 1) * QUART)
             nc.vector.tensor_tensor(
-                g_mx[0][:, q * QUART : (q + 1) * QUART, :].rearrange("p (c e) t -> p c t e", e=2),
-                slack[q // 2][:, :, cols].rearrange("p t (c e) -> p c t e", e=2),
+                g_bf[q // 2][:, cols, :].rearrange("p (c e) t -> p c t e", e=2),
+                slack[q][:].rearrange("p t (c e) -> p c t e", e=2),
                 wy[q // 2][:, :, cols].rearrange("p t (c e) -> p c t e", e=2),
                 MULT,
             )
@@ -149,7 +170,7 @@ def tile_attend_gsqh_w_kernel(tc, xT, wT, y, wt, xm, offs, out):
         def group_xm(b):
             raw = xm_first[:] if b == 0 else xm_rest[:, :, (b - 1) * P : b * P]
             nc.scalar.copy(
-                xm_mx[0][:, b * P : (b + 1) * P, :].rearrange("p (c e) t -> p c t e", e=4),
+                xm_bf[b][:].rearrange("p (c e) t -> p c t e", e=4),
                 raw.rearrange("p t (c e) -> p c t e", e=4),
             )
 
@@ -157,10 +178,10 @@ def tile_attend_gsqh_w_kernel(tc, xT, wT, y, wt, xm, offs, out):
             cols = slice(b * P, (b + 1) * P)
             nc.tensor.matmul_mx(
                 out=bank[:],
-                lhsT=xm_mx[1][:, cols].bitcast(E4M3),
-                lhsT_scale=xm_mx[2][:, cols],
-                rhs=g_mx[1][:, c0 : c0 + N].bitcast(E5M2),
-                rhs_scale=g_mx[2][:, c0 : c0 + N],
+                lhsT=xm_mx[0][:, cols].bitcast(E4M3),
+                lhsT_scale=xm_mx[1][:, cols],
+                rhs=g_mx[0][:, c0 : c0 + N].bitcast(E5M2),
+                rhs_scale=g_mx[1][:, c0 : c0 + N],
                 start=True,
                 stop=True,
             )
@@ -168,45 +189,44 @@ def tile_attend_gsqh_w_kernel(tc, xT, wT, y, wt, xm, offs, out):
         def scatter(b, values, s0, s1):
             nc.vector.tensor_copy(windows[b][:].indirect(offsets[:, s0 // 16 : s1 // 16]), values)
 
-        quantize(x_mx, 0, 2 * P, E4M3)
-        quantize(x_mx, 2 * P, 4 * P, E4M3)
-        for h in range(2):
-            for u in range(2):
-                score(u, h)
-        group_xm(0)
-        quantize(xm_mx, 0, P, E4M3)
+        for q in range(4):
+            score(q)
         weigh(0)
         weigh(1)
-        slack[0] = sb.tile([P, PACK, HALF], F32, name="slack0")
-        for u in range(2):
-            margins(u, 0)
-            hinge(u, 0)
-        slack[1] = sb.tile([P, PACK, HALF], F32, name="slack1")
-        for u in range(2):
-            margins(u, 1)
-            hinge(u, 1)
+        for q in range(2):
+            margins(q)
+            hinge(q)
+        group_xm(0)
         gradient(0)
+        margins(2)
         gradient(1)
-        quantize(g_mx, 0, QUART, E5M2, shift=HALF)
-        quantize(g_mx, QUART, HALF, E5M2, shift=HALF)
-        early_ps = ps.tile([P, N], F32, name="early_ps", tag="bank00")
-        product(early_ps, 0, 0)
-        early = sb.tile([P, HALF], F32, name="early")
-        nc.scalar.copy(early[:], early_ps[:, HALF:N])
+        quantize(xm_bf[0][:], xm_mx, 0, P, E4M3)
+        quantize(g_bf[0][:], g_mx, HALF, N, E5M2)
+        early_ps = [ps.tile([P, N], F32, name=f"early_ps{b}", tag=f"bank{b}") for b in range(EARLY)]
+        product(early_ps[0], 0, 0)
+        hinge(2)
+        margins(3)
+        hinge(3)
+        early0 = sb.tile([P, HALF], F32, name="early0")
+        nc.scalar.copy(early0[:], early_ps[0][:, HALF:N])
         group_xm(1)
         gradient(2)
+        quantize(xm_bf[1][:], xm_mx, P, 2 * P, E4M3)
+        product(early_ps[1], 1, 0)
         gradient(3)
-        quantize(xm_mx, P, 2 * P, E4M3)
-        quantize(g_mx, HALF, N, E5M2, shift=HALF)
-        scatter(0, early[:], 0, HALF)
+        quantize(g_bf[1][:], g_mx, N, N + HALF, E5M2)
+        scatter(0, early0[:], 0, HALF)
+        early1 = sb.tile([P, HALF], F32, name="early1", tag="slack3")
+        nc.scalar.copy(early1[:], early_ps[1][:, HALF:N])
+        scatter(1, early1[:], 0, HALF)
 
         for b in range(BLOCKS):
             if b > 1:
                 group_xm(b)
-                quantize(xm_mx, b * P, (b + 1) * P, E4M3)
+                quantize(xm_bf[b][:], xm_mx, b * P, (b + 1) * P, E4M3)
             dw_ps = ps.tile([P, N], F32, name=f"dw_ps{b}")
             product(dw_ps, b, HALF)
-            s0 = HALF if b == 0 else 0
+            s0 = HALF if b < EARLY else 0
             dw = sb.tile([P, N - s0], F32, name=f"dw{b}")
             nc.scalar.copy(dw[:], dw_ps[:, s0:N])
             scatter(b, dw[:], s0, N)

@@ -71,7 +71,8 @@ def tile_attend_gsqh_w_kernel(tc, xT, wT, y, wt, xm, offs, out):
                 in_=grouped.rearrange("p c j -> p (c j)"),
             )
 
-        w_mx, x_mx, xm_mx = mx_tiles("w", N), mx_tiles("x", R), mx_tiles("xm", D)
+        x_mx, xm_mx = mx_tiles("x", R), mx_tiles("xm", D)
+        w_mx = [mx_tiles("w0", QUART)]
         g_mx = mx_tiles("g", HALF + N)
         w_bf = [grouped_tile("w0", HALF)]
         x_bf = [grouped_tile(f"x{u}", 2 * P) for u in range(2)]
@@ -105,7 +106,7 @@ def tile_attend_gsqh_w_kernel(tc, xT, wT, y, wt, xm, offs, out):
         gather(3, 0, HALF)
         gather(3, HALF, N)
         nc.vector.tensor_copy(*interleaved(0, 2, 4))
-        quantize(w_bf[0][:], w_mx, 0, HALF, E4M3)
+        quantize(w_bf[0][:, 0:QUART, :], w_mx[0], 0, QUART, E4M3)
 
         def dealt(h, u):
             dst = x_bf[u][:].rearrange("p (t m) j -> p m j t", t=2)[:, h * P // 2 : (h + 1) * P // 2]
@@ -116,11 +117,18 @@ def tile_attend_gsqh_w_kernel(tc, xT, wT, y, wt, xm, offs, out):
             nc.scalar.copy(*dealt(0, u))
         for u in range(2):
             nc.vector.tensor_copy(*dealt(1, u))
-        for u in range(2):
-            quantize(x_bf[u][:], x_mx, 2 * u * P, 2 * (u + 1) * P, E4M3)
+        for t in range(PACK):
+            quantize(x_bf[t // 2][:, (t % 2) * P : (t % 2 + 1) * P, :], x_mx, t * P, (t + 1) * P, E4M3)
+        w_mx.append(
+            (
+                sb.tile([P, N - QUART], U32, name="w1_codes", tag="x_raw1", align_bytes=64),
+                sb.tile([P, N - QUART], U8, name="w1_scales", align_bytes=64),
+            )
+        )
+        quantize(w_bf[0][:, QUART:HALF, :], w_mx[1], 0, QUART, E4M3)
         w_bf.append(sb.tile([P, HALF, PACK], BF16, name="w1_bf", tag="x_raw0", align_bytes=64))
         nc.scalar.copy(*interleaved(1, 0, PACK))
-        quantize(w_bf[1][:], w_mx, HALF, N, E4M3)
+        quantize(w_bf[1][:], w_mx[1], QUART, N - QUART, E4M3)
 
         scores = {}
         wy = [sb.tile([P, PACK, HALF], F32, name=f"wy{h}") for h in range(2)]
@@ -128,7 +136,8 @@ def tile_attend_gsqh_w_kernel(tc, xT, wT, y, wt, xm, offs, out):
         slack = {}
 
         def score(q):
-            cols = slice(q * QUART, (q + 1) * QUART)
+            w_codes, w_scales = w_mx[min(q, 1)]
+            cols = slice(max(q - 1, 0) * QUART, max(q, 1) * QUART)
             scores[q] = ps.tile([P, PACK, QUART], F32, name=f"scores{q}", tag=f"bank{q}")
             for t in range(PACK):
                 rows = slice(t * P, (t + 1) * P)
@@ -136,8 +145,8 @@ def tile_attend_gsqh_w_kernel(tc, xT, wT, y, wt, xm, offs, out):
                     out=scores[q][:, t, :],
                     lhsT=x_mx[0][:, rows].bitcast(E4M3),
                     lhsT_scale=x_mx[1][:, rows],
-                    rhs=w_mx[0][:, cols].bitcast(E4M3),
-                    rhs_scale=w_mx[1][:, cols],
+                    rhs=w_codes[:, cols].bitcast(E4M3),
+                    rhs_scale=w_scales[:, cols],
                     start=True,
                     stop=True,
                 )

@@ -109,8 +109,8 @@ def tile_attend_gsqh_w_kernel(tc, xT, wT, y, wt, xm, offs, out):
         quantize(w_bf[0][:, 0:QUART, :], w_mx[0], 0, QUART, E4M3)
 
         def dealt(h, u):
-            dst = x_bf[u][:].rearrange("p (t m) j -> p m j t", t=2)[:, h * P // 2 : (h + 1) * P // 2]
-            src = x_raw[h][:].rearrange("p j (m t) -> p m j t", t=PACK)[:, :, :, 2 * u : 2 * u + 2]
+            dst = x_bf[u][:].rearrange("p (t m e) j -> p m j e t", t=2, e=2)[:, h * P // 4 : (h + 1) * P // 4]
+            src = x_raw[h][:].rearrange("p j (m e t) -> p m j e t", e=2, t=PACK)[:, :, :, :, 2 * u : 2 * u + 2]
             return dst, src
 
         for u in range(2):

@@ -56,7 +56,7 @@ def tile_attend_gsqh_w_kernel(tc, xT, wT, y, wt, xm, offs, out):
         nc.sync.dma_start(xm_rest[:], xm_rows[:, :, P:D])
 
         def grouped_tile(label, columns):
-            return sb.tile([P, columns, PACK], BF16, name=f"{label}_bf", align_bytes=64)
+            return sb.tile([P, columns, PACK], BF16, name=f"{label}_bf", tag=f"{label}_bf", align_bytes=64)
 
         def mx_tiles(label, words):
             codes = sb.tile([P, words], U32, name=f"{label}_codes", align_bytes=64)
@@ -74,9 +74,9 @@ def tile_attend_gsqh_w_kernel(tc, xT, wT, y, wt, xm, offs, out):
         x_mx, xm_mx = mx_tiles("x", R), mx_tiles("xm", D)
         w_mx = [mx_tiles("w0", QUART)]
         g_mx = mx_tiles("g", HALF + N)
-        w_bf = [grouped_tile("w0", HALF)]
-        x_bf = [grouped_tile(f"x{u}", 2 * P) for u in range(2)]
-        xm_bf = [grouped_tile(f"xm{b}", P) for b in range(BLOCKS)]
+        w_bf = [grouped_tile(f"w{h}", HALF) for h in range(2)]
+        x_bf = [[grouped_tile(f"x{h}{u}", P) for u in range(2)] for h in range(2)]
+        xm_bf = [grouped_tile(f"xm{b}", P) for b in range(EARLY)]
         g_bf = [grouped_tile(f"g{h}", HALF) for h in range(2)]
 
         nc.gpsimd.memset(g_mx[0][:, 0:HALF], 0)
@@ -101,24 +101,34 @@ def tile_attend_gsqh_w_kernel(tc, xT, wT, y, wt, xm, offs, out):
 
         gather(0, 0, N)
         gather(1, 0, N)
-        nc.scalar.copy(*interleaved(0, 0, 2))
+        for h in range(2):
+            nc.scalar.copy(*interleaved(h, 0, 2))
         gather(2, 0, N)
         gather(3, 0, HALF)
         gather(3, HALF, N)
-        nc.vector.tensor_copy(*interleaved(0, 2, 4))
+        for h in range(2):
+            nc.vector.tensor_copy(*interleaved(h, 2, 4))
         quantize(w_bf[0][:, 0:QUART, :], w_mx[0], 0, QUART, E4M3)
 
         def dealt(h, u):
-            dst = x_bf[u][:].rearrange("p (t m e) j -> p m j e t", t=2, e=2)[:, h * P // 4 : (h + 1) * P // 4]
+            dst = x_bf[h][u][:].rearrange("p (t m e) j -> p m j e t", t=2, e=2)
             src = x_raw[h][:].rearrange("p j (m e t) -> p m j e t", e=2, t=PACK)[:, :, :, :, 2 * u : 2 * u + 2]
             return dst, src
 
+        def quantize_x(h, t):
+            c0 = t * P + h * P // 2
+            quantize(x_bf[h][t // 2][:, (t % 2) * P // 2 : (t % 2 + 1) * P // 2, :], x_mx, c0, c0 + P // 2, E4M3)
+
         for u in range(2):
             nc.scalar.copy(*dealt(0, u))
-        for u in range(2):
-            nc.vector.tensor_copy(*dealt(1, u))
+        for t in range(2):
+            quantize_x(0, t)
+        nc.vector.tensor_copy(*dealt(1, 0))
+        nc.scalar.copy(*dealt(1, 1))
+        for t in range(2, PACK):
+            quantize_x(0, t)
         for t in range(PACK):
-            quantize(x_bf[t // 2][:, (t % 2) * P : (t % 2 + 1) * P, :], x_mx, t * P, (t + 1) * P, E4M3)
+            quantize_x(1, t)
         w_mx.append(
             (
                 sb.tile([P, N - QUART], U32, name="w1_codes", tag="x_raw1", align_bytes=64),
@@ -126,8 +136,6 @@ def tile_attend_gsqh_w_kernel(tc, xT, wT, y, wt, xm, offs, out):
             )
         )
         quantize(w_bf[0][:, QUART:HALF, :], w_mx[1], 0, QUART, E4M3)
-        w_bf.append(sb.tile([P, HALF, PACK], BF16, name="w1_bf", tag="x_raw0", align_bytes=64))
-        nc.scalar.copy(*interleaved(1, 0, PACK))
         quantize(w_bf[1][:], w_mx[1], QUART, N - QUART, E4M3)
 
         scores = {}
@@ -151,27 +159,27 @@ def tile_attend_gsqh_w_kernel(tc, xT, wT, y, wt, xm, offs, out):
                     stop=True,
                 )
 
-        def weigh(h):
-            for t in range(PACK):
-                if h == 0:
-                    nc.scalar.activation(wy[h][:, t, :], y_sb[h][:, t, :], COPY, scale=neg_wt[:, t : t + 1])
-                else:
-                    nc.gpsimd.tensor_scalar(wy[h][:, t, :], y_sb[h][:, t, :], neg_wt[:, t : t + 1], 0.0, MULT, ADD)
+        def weigh(h, t, on_scalar):
+            if on_scalar:
+                nc.scalar.activation(wy[h][:, t, :], y_sb[h][:, t, :], COPY, scale=neg_wt[:, t : t + 1])
+            else:
+                nc.gpsimd.tensor_scalar(wy[h][:, t, :], y_sb[h][:, t, :], neg_wt[:, t : t + 1], 0.0, MULT, ADD)
 
         def margins(q):
             cols = slice((q % 2) * QUART, (q % 2 + 1) * QUART)
-            margin[q] = sb.tile([P, PACK, QUART], F32, name=f"margin{q}")
+            margin[q] = sb.tile([P, PACK, QUART], F32, name=f"margin{q}", tag="slack1" if q == 3 else f"margin{q}", align_bytes=64)
             nc.vector.tensor_tensor(margin[q][:], scores[q][:], y_sb[q // 2][:, :, cols], MULT)
 
-        def hinge(q):
-            slack[q] = sb.tile([P, PACK, QUART], F32, name=f"slack{q}", tag=f"slack{q}")
-            nc.scalar.activation(slack[q][:], margin[q][:], RELU, bias=1.0, scale=-1.0)
+        def hinge(q, c0=0, c1=QUART):
+            if q not in slack:
+                slack[q] = sb.tile([P, PACK, QUART], F32, name=f"slack{q}", tag=f"slack{q}", align_bytes=64)
+            nc.scalar.activation(slack[q][:, :, c0:c1], margin[q][:, :, c0:c1], RELU, bias=1.0, scale=-1.0)
 
-        def gradient(q):
-            cols = slice((q % 2) * QUART, (q % 2 + 1) * QUART)
-            nc.vector.tensor_tensor(
+        def gradient(q, engine, c0=0, c1=QUART):
+            cols = slice((q % 2) * QUART + c0, (q % 2) * QUART + c1)
+            engine.tensor_tensor(
                 g_bf[q // 2][:, cols, :].rearrange("p (c e) t -> p c t e", e=2),
-                slack[q][:].rearrange("p t (c e) -> p c t e", e=2),
+                slack[q][:, :, c0:c1].rearrange("p t (c e) -> p c t e", e=2),
                 wy[q // 2][:, :, cols].rearrange("p t (c e) -> p c t e", e=2),
                 MULT,
             )
@@ -200,39 +208,48 @@ def tile_attend_gsqh_w_kernel(tc, xT, wT, y, wt, xm, offs, out):
 
         for q in range(4):
             score(q)
-        weigh(0)
-        weigh(1)
+        for t in range(PACK):
+            weigh(0, t, True)
+        for t in range(2):
+            weigh(1, t, False)
         for q in range(2):
             margins(q)
             hinge(q)
-        group_xm(0)
-        gradient(0)
         margins(2)
-        gradient(1)
+        group_xm(0)
+        gradient(0, nc.vector)
+        gradient(1, nc.vector)
         quantize(xm_bf[0][:], xm_mx, 0, P, E4M3)
         quantize(g_bf[0][:], g_mx, HALF, N, E5M2)
         early_ps = [ps.tile([P, N], F32, name=f"early_ps{b}", tag=f"bank{b}") for b in range(EARLY)]
         product(early_ps[0], 0, 0)
         hinge(2)
+        for t in range(2, PACK):
+            weigh(1, t, True)
         margins(3)
-        hinge(3)
+        group_xm(1)
+        hinge(3, 0, QUART // 2)
         early0 = sb.tile([P, HALF], F32, name="early0")
         nc.scalar.copy(early0[:], early_ps[0][:, HALF:N])
-        group_xm(1)
-        gradient(2)
+        hinge(3, QUART // 2, QUART)
         quantize(xm_bf[1][:], xm_mx, P, 2 * P, E4M3)
         product(early_ps[1], 1, 0)
-        gradient(3)
-        quantize(g_bf[1][:], g_mx, N, N + HALF, E5M2)
+        gradient(2, nc.vector)
         scatter(0, early0[:], 0, HALF)
-        early1 = sb.tile([P, HALF], F32, name="early1", tag="slack3")
+        gradient(3, nc.gpsimd, 0, QUART // 2)
+        gradient(3, nc.gpsimd, QUART // 2, QUART)
+        quantize(g_bf[1][:], g_mx, N, N + HALF, E5M2)
+        xm_late = sb.tile([P, D - EARLY * P, PACK], BF16, name="xm_late", tag="slack1", align_bytes=64)
+        nc.scalar.copy(
+            xm_late[:].rearrange("p (c e) t -> p c t e", e=4),
+            xm_rest[:, :, (EARLY - 1) * P :].rearrange("p t (c e) -> p c t e", e=4),
+        )
+        quantize(xm_late[:], xm_mx, EARLY * P, D, E4M3)
+        early1 = sb.tile([P, HALF], F32, name="early1", tag="slack3", align_bytes=64)
         nc.scalar.copy(early1[:], early_ps[1][:, HALF:N])
         scatter(1, early1[:], 0, HALF)
 
         for b in range(BLOCKS):
-            if b > 1:
-                group_xm(b)
-                quantize(xm_bf[b][:], xm_mx, b * P, (b + 1) * P, E4M3)
             dw_ps = ps.tile([P, N], F32, name=f"dw_ps{b}")
             product(dw_ps, b, HALF)
             s0 = HALF if b < EARLY else 0

@@ -139,7 +139,7 @@ def tile_attend_gsqh_w_kernel(tc, xT, wT, y, wt, xm, offs, out):
         quantize(w_bf[1][:], w_mx[1], QUART, N - QUART, E4M3)
 
         scores = {}
-        wy = [sb.tile([P, PACK, HALF], F32, name=f"wy{h}") for h in range(2)]
+        wy = [sb.tile([P, PACK, HALF], F32, name=f"wy{h}", tag=f"wy{h}", align_bytes=64) for h in range(2)]
         margin = {}
         slack = {}
 
@@ -235,19 +235,19 @@ def tile_attend_gsqh_w_kernel(tc, xT, wT, y, wt, xm, offs, out):
         quantize(xm_bf[1][:], xm_mx, P, 2 * P, E4M3)
         product(early_ps[1], 1, 0)
         gradient(2, nc.vector)
+        gradient(3, nc.vector, 0, QUART // 2)
         scatter(0, early0[:], 0, HALF)
-        gradient(3, nc.gpsimd, 0, QUART // 2)
         gradient(3, nc.gpsimd, QUART // 2, QUART)
         quantize(g_bf[1][:], g_mx, N, N + HALF, E5M2)
-        xm_late = sb.tile([P, D - EARLY * P, PACK], BF16, name="xm_late", tag="slack1", align_bytes=64)
+        early1 = sb.tile([P, HALF], F32, name="early1", tag="slack3", align_bytes=64)
+        nc.scalar.copy(early1[:], early_ps[1][:, HALF:N])
+        scatter(1, early1[:], 0, HALF)
+        xm_late = sb.tile([P, D - EARLY * P, PACK], BF16, name="xm_late", tag="wy1", align_bytes=64)
         nc.scalar.copy(
             xm_late[:].rearrange("p (c e) t -> p c t e", e=4),
             xm_rest[:, :, (EARLY - 1) * P :].rearrange("p t (c e) -> p c t e", e=4),
         )
         quantize(xm_late[:], xm_mx, EARLY * P, D, E4M3)
-        early1 = sb.tile([P, HALF], F32, name="early1", tag="slack3", align_bytes=64)
-        nc.scalar.copy(early1[:], early_ps[1][:, HALF:N])
-        scatter(1, early1[:], 0, HALF)
 
         for b in range(BLOCKS):
             dw_ps = ps.tile([P, N], F32, name=f"dw_ps{b}")

@@ -187,8 +187,8 @@ def tile_attend_gsqh_w_kernel(tc, xT, wT, y, wt, xm, offs, out):
         def group_xm(b):
             raw = xm_first[:] if b == 0 else xm_rest[:, :, (b - 1) * P : b * P]
             nc.scalar.copy(
-                xm_bf[b][:].rearrange("p (c e) t -> p c t e", e=4),
-                raw.rearrange("p t (c e) -> p c t e", e=4),
+                xm_bf[b][:].rearrange("p (c e) t -> p c t e", e=2),
+                raw.rearrange("p t (c e) -> p c t e", e=2),
             )
 
         def product(bank, b, c0):
@@ -244,8 +244,8 @@ def tile_attend_gsqh_w_kernel(tc, xT, wT, y, wt, xm, offs, out):
         scatter(1, early1[:], 0, HALF)
         xm_late = sb.tile([P, D - EARLY * P, PACK], BF16, name="xm_late", tag="wy1", align_bytes=64)
         nc.scalar.copy(
-            xm_late[:].rearrange("p (c e) t -> p c t e", e=4),
-            xm_rest[:, :, (EARLY - 1) * P :].rearrange("p t (c e) -> p c t e", e=4),
+            xm_late[:].rearrange("p (c e) t -> p c t e", e=2),
+            xm_rest[:, :, (EARLY - 1) * P :].rearrange("p t (c e) -> p c t e", e=2),
         )
         quantize(xm_late[:], xm_mx, EARLY * P, D, E4M3)
 

@@ -256,6 +256,4 @@ def tile_attend_gsqh_w_kernel(tc, xT, wT, y, wt, xm, offs, out):
             dw = sb.tile([P, N - s0], F32, name=f"dw{b}")
             nc.scalar.copy(dw[:], dw_ps[:, s0:N])
             scatter(b, dw[:], s0, N)
-            nc.sync.dma_start(out[b * P : (b + 1) * P, 0 : T // 2], windows[b][:, 0 : T // 2])
-            second = nc.scalar if b == BLOCKS - 1 else nc.sync
-            second.dma_start(out[b * P : (b + 1) * P, T // 2 : T], windows[b][:, T // 2 : T])
+            nc.sync.dma_start(out[b * P : (b + 1) * P, :], windows[b][:])

@@ -33,7 +33,8 @@ def tile_attend_gsqh_w_kernel(tc, xT, wT, y, wt, xm, offs, out):
 
         offsets = sb.tile([P, N // 16], U16, name="offsets")
         wt_sb = sb.tile([P, PACK], F32, name="wt_sb")
-        planes = [sb.tile([P, T], F32, name=f"plane{j}") for j in range(PACK)]
+        first_planes = sb.tile([P, 2, T], F32, name="first_planes")
+        planes = [first_planes[:, j, :] for j in range(2)] + [sb.tile([P, T], F32, name=f"plane{j}")[:] for j in range(2, PACK)]
         x_raw = [sb.tile([P, PACK, R // 2], F32, name=f"x_raw{h}", tag=f"x_raw{h}", align_bytes=64) for h in range(2)]
         y_sb = [sb.tile([P, PACK, HALF], F32, name=f"y_sb{h}") for h in range(2)]
         xm_first = sb.tile([P, PACK, P], F32, name="xm_first")
@@ -41,11 +42,11 @@ def tile_attend_gsqh_w_kernel(tc, xT, wT, y, wt, xm, offs, out):
 
         w_rows = wT.rearrange("(p j) c -> p j c", j=PACK)
         y_rows = y[0].rearrange("(p t) i -> p t i", t=PACK)
-        nc.sync.dma_start(planes[0][:], w_rows[:, 0, :])
+        nc.sync.dma_start(first_planes[:], w_rows[:, 0:2, :])
         nc.sync.dma_start(offsets[:], offs)
         nc.scalar.dma_start(wt_sb[:], wt[0].rearrange("(p t) o -> p (t o)", t=PACK))
-        for j in range(1, PACK):
-            nc.sync.dma_start(planes[j][:], w_rows[:, j, :])
+        for j in range(2, PACK):
+            nc.sync.dma_start(planes[j], w_rows[:, j, :])
         x_rows = xT[0].rearrange("(p j) r -> p j r", j=PACK)
         for h in range(2):
             nc.sync.dma_start(x_raw[h][:], x_rows[:, :, h * R // 2 : (h + 1) * R // 2])
@@ -92,7 +93,7 @@ def tile_attend_gsqh_w_kernel(tc, xT, wT, y, wt, xm, offs, out):
         picked = sb.tile([P, PACK, N], F32, name="picked")
 
         def gather(j, s0, s1):
-            nc.vector.tensor_copy(picked[:, j, s0:s1], planes[j][:].indirect(offsets[:, s0 // 16 : s1 // 16]))
+            nc.vector.tensor_copy(picked[:, j, s0:s1], planes[j].indirect(offsets[:, s0 // 16 : s1 // 16]))
 
         def interleaved(h, j0, j1):
             dst = w_bf[h][:, :, j0:j1].rearrange("p (c e) j -> p c j e", e=4)

@@ -76,7 +76,8 @@ def tile_attend_gsqh_w_kernel(tc, xT, wT, y, wt, xm, offs, out):
         w_mx = [mx_tiles("w0", QUART)]
         g_mx = mx_tiles("g", HALF + N)
         w_bf = [grouped_tile(f"w{h}", HALF) for h in range(2)]
-        x_bf = [[grouped_tile(f"x{h}{u}", P) for u in range(2)] for h in range(2)]
+        x_low = sb.tile([P, 2, P, PACK], BF16, name="x_low", align_bytes=64)
+        x_high = [sb.tile([P, 2, P // 2, PACK], BF16, name=f"x_high{h}", align_bytes=64) for h in range(2)]
         xm_bf = [grouped_tile(f"xm{b}", P) for b in range(EARLY)]
         g_bf = [grouped_tile(f"g{h}", HALF) for h in range(2)]
 
@@ -109,27 +110,23 @@ def tile_attend_gsqh_w_kernel(tc, xT, wT, y, wt, xm, offs, out):
         gather(3, HALF, N)
         for h in range(2):
             nc.vector.tensor_copy(*interleaved(h, 2, 4))
-        quantize(w_bf[0][:, 0:QUART, :], w_mx[0], 0, QUART, E4M3)
 
         def dealt(h, u):
-            dst = x_bf[h][u][:].rearrange("p (t m e) j -> p m j e t", t=2, e=2)
+            dst = x_high[h][:] if u else x_low[:, :, h * P // 2 : (h + 1) * P // 2, :]
             src = x_raw[h][:].rearrange("p j (m e t) -> p m j e t", e=2, t=PACK)[:, :, :, :, 2 * u : 2 * u + 2]
-            return dst, src
-
-        def quantize_x(h, t):
-            c0 = t * P + h * P // 2
-            quantize(x_bf[h][t // 2][:, (t % 2) * P // 2 : (t % 2 + 1) * P // 2, :], x_mx, c0, c0 + P // 2, E4M3)
+            return dst.rearrange("p t (m e) j -> p m j e t", e=2), src
 
         for u in range(2):
             nc.scalar.copy(*dealt(0, u))
-        for t in range(2):
-            quantize_x(0, t)
         nc.vector.tensor_copy(*dealt(1, 0))
         nc.scalar.copy(*dealt(1, 1))
-        for t in range(2, PACK):
-            quantize_x(0, t)
-        for t in range(PACK):
-            quantize_x(1, t)
+        quantize(w_bf[0][:, 0:QUART, :], w_mx[0], 0, QUART, E4M3)
+        for t in range(2):
+            quantize(x_low[:, t, :, :], x_mx, t * P, (t + 1) * P, E4M3)
+        for h in range(2):
+            for t in range(2, PACK):
+                c0 = t * P + h * P // 2
+                quantize(x_high[h][:, t - 2, :, :], x_mx, c0, c0 + P // 2, E4M3)
         w_mx.append(
             (
                 sb.tile([P, N - QUART], U32, name="w1_codes", tag="x_raw1", align_bytes=64),

@@ -90,6 +90,8 @@ def tile_attend_gsqh_w_kernel(tc, xT, wT, y, wt, xm, offs, out):
 
         neg_wt = sb.tile([P, PACK], F32, name="neg_wt")
         nc.scalar.activation(neg_wt[:], wt_sb[:], COPY, scale=-1.0)
+        one = sb.tile([P, 1], F32, name="one", tag="early1")
+        nc.gpsimd.memset(one[:], 1.0)
 
         picked = sb.tile([P, PACK, N], F32, name="picked")
 
@@ -168,10 +170,10 @@ def tile_attend_gsqh_w_kernel(tc, xT, wT, y, wt, xm, offs, out):
             margin[q] = sb.tile([P, PACK, QUART], F32, name=f"margin{q}", tag="slack1" if q == 3 else f"margin{q}", align_bytes=64)
             nc.vector.tensor_tensor(margin[q][:], scores[q][:], y_sb[q // 2][:, :, cols], MULT)
 
-        def hinge(q, c0=0, c1=QUART):
+        def hinge(q, c0=0, c1=QUART, bias=1.0):
             if q not in slack:
                 slack[q] = sb.tile([P, PACK, QUART], F32, name=f"slack{q}", tag=f"slack{q}", align_bytes=64)
-            nc.scalar.activation(slack[q][:, :, c0:c1], margin[q][:, :, c0:c1], RELU, bias=1.0, scale=-1.0)
+            nc.scalar.activation(slack[q][:, :, c0:c1], margin[q][:, :, c0:c1], RELU, bias=bias, scale=-1.0)
 
         def gradient(q, engine, c0=0, c1=QUART):
             cols = slice((q % 2) * QUART + c0, (q % 2) * QUART + c1)
@@ -229,7 +231,7 @@ def tile_attend_gsqh_w_kernel(tc, xT, wT, y, wt, xm, offs, out):
         hinge(3, 0, QUART // 2)
         early0 = sb.tile([P, HALF], F32, name="early0")
         nc.scalar.copy(early0[:], early_ps[0][:, HALF:N])
-        hinge(3, QUART // 2, QUART)
+        hinge(3, QUART // 2, QUART, one[:])
         quantize(xm_bf[1][:], xm_mx, P, 2 * P, E4M3)
         product(early_ps[1], 1, 0)
         gradient(2, nc.vector)
@@ -237,14 +239,19 @@ def tile_attend_gsqh_w_kernel(tc, xT, wT, y, wt, xm, offs, out):
         scatter(0, early0[:], 0, HALF)
         gradient(3, nc.gpsimd, QUART // 2, QUART)
         quantize(g_bf[1][:], g_mx, N, N + HALF, E5M2)
-        early1 = sb.tile([P, HALF], F32, name="early1", tag="slack3", align_bytes=64)
+        xm_late = sb.tile([P, D - EARLY * P, PACK], BF16, name="xm_late", tag="slack1", align_bytes=64)
+
+        def group_late(b):
+            nc.scalar.copy(
+                xm_late[:, (b - EARLY) * P : (b - EARLY + 1) * P, :].rearrange("p (c e) t -> p c t e", e=2),
+                xm_rest[:, :, (b - 1) * P : b * P].rearrange("p t (c e) -> p c t e", e=2),
+            )
+
+        group_late(2)
+        early1 = sb.tile([P, HALF], F32, name="early1", tag="early1")
         nc.scalar.copy(early1[:], early_ps[1][:, HALF:N])
         scatter(1, early1[:], 0, HALF)
-        xm_late = sb.tile([P, D - EARLY * P, PACK], BF16, name="xm_late", tag="wy1", align_bytes=64)
-        nc.scalar.copy(
-            xm_late[:].rearrange("p (c e) t -> p c t e", e=2),
-            xm_rest[:, :, (EARLY - 1) * P :].rearrange("p t (c e) -> p c t e", e=2),
-        )
+        group_late(3)
         quantize(xm_late[:], xm_mx, EARLY * P, D, E4M3)
 
         for b in range(BLOCKS):

@@ -99,8 +99,8 @@ def tile_attend_gsqh_w_kernel(tc, xT, wT, y, wt, xm, offs, out):
             nc.vector.tensor_copy(picked[:, j, s0:s1], planes[j].indirect(offsets[:, s0 // 16 : s1 // 16]))
 
         def interleaved(h, j0, j1):
-            dst = w_bf[h][:, :, j0:j1].rearrange("p (c e) j -> p c j e", e=4)
-            src = picked[:, j0:j1, h * HALF : (h + 1) * HALF].rearrange("p j (c e) -> p c j e", e=4)
+            dst = w_bf[h][:, :, j0:j1].rearrange("p (c e) j -> p c j e", e=2)
+            src = picked[:, j0:j1, h * HALF : (h + 1) * HALF].rearrange("p j (c e) -> p c j e", e=2)
             return dst, src
 
         gather(0, 0, N)

from contextlib import ExitStack

import concourse.mybir as mybir

D, T, R, N = 512, 2048, 512, 512
FLOPS = 2 * 2 * D * R * N

F32 = mybir.dt.float32
BF16 = mybir.dt.bfloat16
U32 = mybir.dt.uint32
U16 = mybir.dt.uint16
U8 = mybir.dt.uint8
E4M3 = mybir.dt.float8_e4m3fn_x4
E5M2 = mybir.dt.float8_e5m2_x4
COPY = mybir.ActivationFunctionType.Copy
RELU = mybir.ActivationFunctionType.Relu
MULT = mybir.AluOpType.mult
ADD = mybir.AluOpType.add

P = 128
PACK = 4
HALF = N // 2
BLOCKS = D // P
QUART = N // 4
EARLY = 2


def tile_attend_gsqh_w_kernel(tc, xT, wT, y, wt, xm, offs, out):
    nc = tc.nc
    with ExitStack() as ctx:
        sb = ctx.enter_context(tc.tile_pool(name="sb", bufs=1))
        ps = ctx.enter_context(tc.psum_pool(name="ps", bufs=1))

        offsets = sb.tile([P, N // 16], U16, name="offsets")
        wt_sb = sb.tile([P, PACK], F32, name="wt_sb")
        first_planes = sb.tile([P, 2, T], F32, name="first_planes")
        planes = [first_planes[:, j, :] for j in range(2)] + [sb.tile([P, T], F32, name=f"plane{j}")[:] for j in range(2, PACK)]
        x_raw = [sb.tile([P, PACK, R // 2], F32, name=f"x_raw{h}", tag=f"x_raw{h}", align_bytes=64) for h in range(2)]
        y_sb = [sb.tile([P, PACK, HALF], F32, name=f"y_sb{h}") for h in range(2)]
        xm_first = sb.tile([P, PACK, P], F32, name="xm_first")
        xm_rest = sb.tile([P, PACK, D - P], F32, name="xm_rest")

        w_rows = wT.rearrange("(p j) c -> p j c", j=PACK)
        y_rows = y[0].rearrange("(p t) i -> p t i", t=PACK)
        nc.sync.dma_start(first_planes[:], w_rows[:, 0:2, :])
        nc.sync.dma_start(offsets[:], offs)
        nc.scalar.dma_start(wt_sb[:], wt[0].rearrange("(p t) o -> p (t o)", t=PACK))
        for j in range(2, PACK):
            nc.sync.dma_start(planes[j], w_rows[:, j, :])
        x_rows = xT[0].rearrange("(p j) r -> p j r", j=PACK)
        for h in range(2):
            nc.sync.dma_start(x_raw[h][:], x_rows[:, :, h * R // 2 : (h + 1) * R // 2])
        xm_rows = xm[0].rearrange("(p t) d -> p t d", t=PACK)
        for h in range(2):
            nc.sync.dma_start(y_sb[h][:], y_rows[:, :, h * HALF : (h + 1) * HALF])
        nc.sync.dma_start(xm_first[:], xm_rows[:, :, 0:P])
        nc.sync.dma_start(xm_rest[:], xm_rows[:, :, P:D])

        def grouped_tile(label, columns):
            return sb.tile([P, columns, PACK], BF16, name=f"{label}_bf", tag=f"{label}_bf", align_bytes=64)

        def mx_tiles(label, words):
            codes = sb.tile([P, words], U32, name=f"{label}_codes", align_bytes=64)
            scales = sb.tile([P, words], U8, name=f"{label}_scales", align_bytes=64)
            return codes, scales

        def quantize(grouped, tiles, c0, c1, fmt):
            codes, scales = tiles
            nc.vector.quantize_mx(
                out=codes[:, c0:c1].bitcast(fmt),
                scales=scales[:, c0:c1],
                in_=grouped.rearrange("p c j -> p (c j)"),
            )

        x_mx, xm_mx = mx_tiles("x", R), mx_tiles("xm", D)
        w_mx = [mx_tiles("w0", QUART)]
        g_mx = mx_tiles("g", HALF + N)
        w_bf = [grouped_tile(f"w{h}", HALF) for h in range(2)]
        x_low = sb.tile([P, 2, P, PACK], BF16, name="x_low", align_bytes=64)
        x_high = [sb.tile([P, 2, P // 2, PACK], BF16, name=f"x_high{h}", align_bytes=64) for h in range(2)]
        xm_bf = [grouped_tile(f"xm{b}", P) for b in range(EARLY)]
        g_bf = [grouped_tile(f"g{h}", HALF) for h in range(2)]

        nc.gpsimd.memset(g_mx[0][:, 0:HALF], 0)
        nc.gpsimd.memset(g_mx[1][:, 0:HALF], 0)
        windows = [sb.tile([P, T], F32, name=f"window{b}") for b in range(BLOCKS)]
        for b in range(BLOCKS):
            engine = nc.vector if b < 2 else nc.gpsimd
            engine.memset(windows[b][:], 0.0)

        neg_wt = sb.tile([P, PACK], F32, name="neg_wt")
        nc.scalar.activation(neg_wt[:], wt_sb[:], COPY, scale=-1.0)
        one = sb.tile([P, 1], F32, name="one", tag="early1")
        nc.gpsimd.memset(one[:], 1.0)

        picked = sb.tile([P, PACK, N], F32, name="picked")

        def gather(j, s0, s1):
            nc.vector.tensor_copy(picked[:, j, s0:s1], planes[j].indirect(offsets[:, s0 // 16 : s1 // 16]))

        def interleaved(h, j0, j1):
            dst = w_bf[h][:, :, j0:j1].rearrange("p (c e) j -> p c j e", e=2)
            src = picked[:, j0:j1, h * HALF : (h + 1) * HALF].rearrange("p j (c e) -> p c j e", e=2)
            return dst, src

        gather(0, 0, N)
        gather(1, 0, N)
        for h in range(2):
            nc.scalar.copy(*interleaved(h, 0, 2))
        gather(2, 0, N)
        gather(3, 0, HALF)
        gather(3, HALF, N)
        for h in range(2):
            nc.vector.tensor_copy(*interleaved(h, 2, 4))

        def dealt(h, u):
            dst = x_high[h][:] if u else x_low[:, :, h * P // 2 : (h + 1) * P // 2, :]
            src = x_raw[h][:].rearrange("p j (m e t) -> p m j e t", e=2, t=PACK)[:, :, :, :, 2 * u : 2 * u + 2]
            return dst.rearrange("p t (m e) j -> p m j e t", e=2), src

        for u in range(2):
            nc.scalar.copy(*dealt(0, u))
        nc.vector.tensor_copy(*dealt(1, 0))
        nc.scalar.copy(*dealt(1, 1))
        quantize(w_bf[0][:, 0:QUART, :], w_mx[0], 0, QUART, E4M3)
        for t in range(2):
            quantize(x_low[:, t, :, :], x_mx, t * P, (t + 1) * P, E4M3)
        for h in range(2):
            for t in range(2, PACK):
                c0 = t * P + h * P // 2
                quantize(x_high[h][:, t - 2, :, :], x_mx, c0, c0 + P // 2, E4M3)
        w_mx.append(
            (
                sb.tile([P, N - QUART], U32, name="w1_codes", tag="x_raw1", align_bytes=64),
                sb.tile([P, N - QUART], U8, name="w1_scales", align_bytes=64),
            )
        )
        quantize(w_bf[0][:, QUART:HALF, :], w_mx[1], 0, QUART, E4M3)
        quantize(w_bf[1][:], w_mx[1], QUART, N - QUART, E4M3)

        scores = {}
        wy = [sb.tile([P, PACK, HALF], F32, name=f"wy{h}", tag=f"wy{h}", align_bytes=64) for h in range(2)]
        margin = {}
        slack = {}

        def score(q):
            w_codes, w_scales = w_mx[min(q, 1)]
            cols = slice(max(q - 1, 0) * QUART, max(q, 1) * QUART)
            scores[q] = ps.tile([P, PACK, QUART], F32, name=f"scores{q}", tag=f"bank{q}")
            for t in range(PACK):
                rows = slice(t * P, (t + 1) * P)
                nc.tensor.matmul_mx(
                    out=scores[q][:, t, :],
                    lhsT=x_mx[0][:, rows].bitcast(E4M3),
                    lhsT_scale=x_mx[1][:, rows],
                    rhs=w_codes[:, cols].bitcast(E4M3),
                    rhs_scale=w_scales[:, cols],
                    start=True,
                    stop=True,
                )

        def weigh(h, t, on_scalar):
            if on_scalar:
                nc.scalar.activation(wy[h][:, t, :], y_sb[h][:, t, :], COPY, scale=neg_wt[:, t : t + 1])
            else:
                nc.gpsimd.tensor_scalar(wy[h][:, t, :], y_sb[h][:, t, :], neg_wt[:, t : t + 1], 0.0, MULT, ADD)

        def margins(q):
            cols = slice((q % 2) * QUART, (q % 2 + 1) * QUART)
            margin[q] = sb.tile([P, PACK, QUART], F32, name=f"margin{q}", tag="slack1" if q == 3 else f"margin{q}", align_bytes=64)
            nc.vector.tensor_tensor(margin[q][:], scores[q][:], y_sb[q // 2][:, :, cols], MULT)

        def hinge(q, c0=0, c1=QUART, bias=1.0):
            if q not in slack:
                slack[q] = sb.tile([P, PACK, QUART], F32, name=f"slack{q}", tag=f"slack{q}", align_bytes=64)
            nc.scalar.activation(slack[q][:, :, c0:c1], margin[q][:, :, c0:c1], RELU, bias=bias, scale=-1.0)

        def gradient(q, engine, c0=0, c1=QUART):
            cols = slice((q % 2) * QUART + c0, (q % 2) * QUART + c1)
            engine.tensor_tensor(
                g_bf[q // 2][:, cols, :].rearrange("p (c e) t -> p c t e", e=2),
                slack[q][:, :, c0:c1].rearrange("p t (c e) -> p c t e", e=2),
                wy[q // 2][:, :, cols].rearrange("p t (c e) -> p c t e", e=2),
                MULT,
            )

        def group_xm(b):
            raw = xm_first[:] if b == 0 else xm_rest[:, :, (b - 1) * P : b * P]
            nc.scalar.copy(
                xm_bf[b][:].rearrange("p (c e) t -> p c t e", e=2),
                raw.rearrange("p t (c e) -> p c t e", e=2),
            )

        def product(bank, b, c0):
            cols = slice(b * P, (b + 1) * P)
            nc.tensor.matmul_mx(
                out=bank[:],
                lhsT=xm_mx[0][:, cols].bitcast(E4M3),
                lhsT_scale=xm_mx[1][:, cols],
                rhs=g_mx[0][:, c0 : c0 + N].bitcast(E5M2),
                rhs_scale=g_mx[1][:, c0 : c0 + N],
                start=True,
                stop=True,
            )

        def scatter(b, values, s0, s1):
            nc.vector.tensor_copy(windows[b][:].indirect(offsets[:, s0 // 16 : s1 // 16]), values)

        for q in range(4):
            score(q)
        for t in range(PACK):
            weigh(0, t, True)
        for t in range(2):
            weigh(1, t, False)
        for q in range(2):
            margins(q)
            hinge(q)
        margins(2)
        group_xm(0)
        gradient(0, nc.vector)
        gradient(1, nc.vector)
        quantize(xm_bf[0][:], xm_mx, 0, P, E4M3)
        quantize(g_bf[0][:], g_mx, HALF, N, E5M2)
        early_ps = [ps.tile([P, N], F32, name=f"early_ps{b}", tag=f"bank{b}") for b in range(EARLY)]
        product(early_ps[0], 0, 0)
        hinge(2)
        for t in range(2, PACK):
            weigh(1, t, True)
        margins(3)
        group_xm(1)
        hinge(3, 0, QUART // 2)
        early0 = sb.tile([P, HALF], F32, name="early0")
        nc.scalar.copy(early0[:], early_ps[0][:, HALF:N])
        hinge(3, QUART // 2, QUART, one[:])
        quantize(xm_bf[1][:], xm_mx, P, 2 * P, E4M3)
        product(early_ps[1], 1, 0)
        gradient(2, nc.vector)
        gradient(3, nc.vector, 0, QUART // 2)
        scatter(0, early0[:], 0, HALF)
        gradient(3, nc.gpsimd, QUART // 2, QUART)
        quantize(g_bf[1][:], g_mx, N, N + HALF, E5M2)
        xm_late = sb.tile([P, D - EARLY * P, PACK], BF16, name="xm_late", tag="slack1", align_bytes=64)

        def group_late(b):
            nc.scalar.copy(
                xm_late[:, (b - EARLY) * P : (b - EARLY + 1) * P, :].rearrange("p (c e) t -> p c t e", e=2),
                xm_rest[:, :, (b - 1) * P : b * P].rearrange("p t (c e) -> p c t e", e=2),
            )

        group_late(2)
        early1 = sb.tile([P, HALF], F32, name="early1", tag="early1")
        nc.scalar.copy(early1[:], early_ps[1][:, HALF:N])
        scatter(1, early1[:], 0, HALF)
        group_late(3)
        quantize(xm_late[:], xm_mx, EARLY * P, D, E4M3)

        for b in range(BLOCKS):
            dw_ps = ps.tile([P, N], F32, name=f"dw_ps{b}")
            product(dw_ps, b, HALF)
            s0 = HALF if b < EARLY else 0
            dw = sb.tile([P, N - s0], F32, name=f"dw{b}")
            nc.scalar.copy(dw[:], dw_ps[:, s0:N])
            scatter(b, dw[:], s0, N)
            nc.sync.dma_start(out[b * P : (b + 1) * P, :], windows[b][:])
